import numpy as np
import ml_dtypes


def mxq(x, axis, fmt="e4m3"):
    dtype, down = {"e4m3": (ml_dtypes.float8_e4m3fn, 7), "e5m2": (ml_dtypes.float8_e5m2, 14)}[fmt]
    v = np.moveaxis(np.asarray(x, np.float32).astype(ml_dtypes.bfloat16).astype(np.float64), axis, -1)
    blocks = v.reshape(v.shape[:-1] + (-1, 32))
    amax = np.abs(blocks).max(-1, keepdims=True)
    byte = np.maximum(np.where(amax > 0, np.frexp(amax)[1] - 1 + 127, 0) - down, 1)
    scale = np.exp2(byte - 127.0)
    codes = (blocks / scale).astype(np.float32).astype(dtype).astype(np.float64)
    return np.moveaxis((codes * scale).reshape(v.shape), -1, axis)


WIDE = False


def mx_kscale(k):
    if not WIDE:
        return np.ones(k)
    levels = np.array([10, -10, 5, -5, 0])
    if k % 512:
        return np.exp2(np.random.permutation(np.resize(levels, k // 32))).repeat(32)
    a = np.empty((k // 512, 16))
    for p in range(k // 512):
        a[p, :8] = np.random.permutation(np.resize(levels, 8))
        for g in range(8):
            far = levels[np.abs(levels - a[p, g]) >= 10]
            a[p, g + 8] = far[np.random.randint(len(far))]
    return np.exp2(a.ravel()).repeat(32)


def f64(x):
    return np.asarray(x).astype(np.float64)


def striped8(idx):
    return np.asarray(idx).reshape(8, -1, 16).transpose(0, 2, 1).reshape(128, -1).astype(np.uint16)


def unstriped8(offs):
    return offs.reshape(8, 16, -1).transpose(0, 2, 1).reshape(8, -1).astype(np.int64)


def pick8(x, idx, run):
    r = np.arange(len(x))
    return x[r[:, None], idx[r % (8 * run) // run]]


E2M1 = np.array([0.0, 0.5, 1.0, 1.5, 2.0, 3.0, 4.0, 6.0, -0.0, -0.5, -1.0, -1.5, -2.0, -3.0, -4.0, -6.0])


def pack_weight(w, fmt):
    k, n = w.shape
    w = f64(np.asarray(w, np.float32).astype(ml_dtypes.bfloat16)).reshape(k // 32, 32, n)
    amax = np.abs(w).max(1)
    if fmt == "e4m3":
        byte = np.frexp(amax)[1] - 1 + 127 - 7
    else:
        mant, ex = np.frexp(amax / 6.0)
        byte = np.where(mant > 0.5, ex, ex - 1) + 127
    byte = np.clip(np.where(amax > 0, byte, 1), 1, 254)
    scaled = (w * np.exp2(127.0 - byte)[:, None, :]).reshape(k, n).astype(np.float32)
    by_word = np.ascontiguousarray(scaled.reshape(k // 512, 128, 4, n).transpose(0, 1, 3, 2))
    if fmt == "e4m3":
        words = by_word.astype(ml_dtypes.float8_e4m3fn).view(np.uint8)
    else:
        c = by_word.astype(ml_dtypes.float4_e2m1fn).view(np.uint8) & 0xF
        words = (c[..., 0::2] | (c[..., 1::2] << 4)).reshape(k // 512, 128, 2 * n)
    return np.ascontiguousarray(words), np.ascontiguousarray(byte.astype(np.uint8).reshape(k // 512, 16, n))


def unpack_weight(words, scales, fmt):
    g, _, n = scales.shape
    words = np.ascontiguousarray(words).reshape(g, 128, n, -1)
    if fmt == "e4m3":
        vals = words.view(ml_dtypes.float8_e4m3fn).astype(np.float64)
    else:
        nib = np.empty((g, 128, n, 4), np.uint8)
        nib[..., 0::2] = words & 0xF
        nib[..., 1::2] = words >> 4
        vals = E2M1[nib]
    vals = vals * np.repeat(np.exp2(scales.astype(np.float64) - 127.0), 8, axis=1)[..., None]
    return vals.transpose(0, 1, 3, 2).reshape(g * 512, n)


D, T, I, Q = 512, 1024, 512, 128


def setup_inputs():
    n = np.random.standard_normal
    idx = np.stack([np.random.permutation(T)[:I] for _ in range(8)])
    idx2 = np.stack([np.random.permutation(T)[:I] for _ in range(8)])
    idx3 = np.stack([np.random.permutation(T)[:I] for _ in range(8)])
    fd = mx_kscale(D)
    keysp = pack_weight(n((D, T)) / fd[:, None], "e4m3")
    return {
        "query": (n((D, Q)) * 0.9 / np.sqrt(D) * fd[:, None]).astype(np.float32),
        "query2": (n((D, Q)) * 0.9 / np.sqrt(D) * fd[:, None]).astype(np.float32),
        "keys_words": keysp[0],
        "keys_scales": keysp[1],
        "lam": (np.random.uniform(0.5, 1.3, (Q, 1))).astype(np.float32),
        "old": (1.0 * n((Q, T))).astype(np.float32),
        "offs": striped8(idx),
        "offs2": striped8(idx2),
        "offs3": striped8(idx3),
    }


def reference(query, query2, keys_words, keys_scales, lam, old, offs, offs2, offs3):
    idx = unstriped8(offs)
    idx2 = unstriped8(offs2)
    idx3 = unstriped8(offs3)
    keysu = unpack_weight(keys_words, keys_scales, "e4m3")
    queryq = mxq(f64(query), 0, "e4m3")
    a = queryq.T @ keysu
    query2q = mxq(f64(query2), 0, "e4m3")
    b = query2q.T @ keysu
    w = (np.maximum(pick8(a, idx, 16), pick8(b, idx2, 16)) - np.maximum(pick8(a, idx2, 16), pick8(b, idx, 16))) * f64(lam)
    f1 = np.zeros((Q, T))
    f1[np.arange(Q)[:, None], idx[np.arange(Q) % 128 // 16]] = w
    f2 = f1 + f64(old)
    y = pick8(f2, idx3, 16) * w
    return y

@@ -1,0 +1,141 @@
+from contextlib import ExitStack
+
+import concourse.mybir as mybir
+
+F32 = mybir.dt.float32
+BF16 = mybir.dt.bfloat16
+U32 = mybir.dt.uint32
+I32 = mybir.dt.int32
+U16 = mybir.dt.uint16
+U8 = mybir.dt.uint8
+FP8X4 = mybir.dt.float8_e4m3fn_x4
+ALU = mybir.AluOpType
+COPY = mybir.ActivationFunctionType.Copy
+
+P = 128
+PACK = 4
+D, T, SLOTS, Q = 512, 1024, 512, 128
+HALF = SLOTS // 2
+PER_COL = 16
+
+FLOPS = 2 * 2 * D * Q * T
+
+
+def tile_attend_exchanged_lean_throughtimes_heads_kernel(
+    tc, query, query2, keys_words, keys_scales, lam, old, offs, offs2, offs3, out
+):
+    nc = tc.nc
+    with ExitStack() as ctx:
+        sb = ctx.enter_context(tc.tile_pool(name="sb", bufs=1))
+        ps = ctx.enter_context(tc.psum_pool(name="ps", bufs=1))
+
+        raw = [sb.tile([P, PACK, Q], F32, name="raw%d" % j) for j in range(2)]
+        key_words = sb.tile([P, T], U32, name="key_words", align_bytes=64)
+        scale_rows = sb.tile([P, T // 4], U32, name="scale_rows")
+        nc.sync.dma_start(out=raw[0][:], in_=query.rearrange("(p r) q -> p r q", r=PACK))
+        for quad in range(4):
+            nc.sync.dma_start(
+                out=scale_rows[32 * quad : 32 * quad + 4, :].bitcast(I32),
+                in_=keys_scales[0][4 * quad : 4 * quad + 4, :].bitcast(I32),
+            )
+        nc.sync.dma_start(
+            out=key_words[:].bitcast(I32), in_=keys_words[0].rearrange("p n r -> p (n r)").bitcast(I32)
+        )
+        nc.sync.dma_start(out=raw[1][:], in_=query2.rearrange("(p r) q -> p r q", r=PACK))
+        lam_col = sb.tile([P, 1], F32, name="lam_col")
+        list1 = sb.tile([P, SLOTS // PER_COL], U16, name="list1")
+        list2 = sb.tile([P, SLOTS // PER_COL], U16, name="list2")
+        list3 = sb.tile([P, SLOTS // PER_COL], U16, name="list3")
+        old_sb = sb.tile([P, T], F32, name="old_sb")
+        nc.sync.dma_start(out=lam_col[:], in_=lam)
+        nc.sync.dma_start(list1[:], offs)
+        nc.sync.dma_start(list2[:], offs2)
+        nc.sync.dma_start(out=old_sb[:], in_=old)
+        nc.sync.dma_start(list3[:], offs3)
+
+        key_scales = sb.tile([P, T], U8, name="key_scales", align_bytes=64)
+        nc.vector.memset(key_scales[:].bitcast(U32), 0)
+        f1 = sb.tile([P, T], F32, name="f1")
+        nc.vector.memset(f1[:], 0.0)
+        for quad in range(4):
+            rows = slice(32 * quad, 32 * quad + 4)
+            nc.vector.tensor_copy(out=key_scales[rows, :].bitcast(I32), in_=scale_rows[rows, :].bitcast(I32))
+
+        def cols(lst, lo, hi):
+            return lst[:, lo // PER_COL : hi // PER_COL]
+
+        codes, scales = [], []
+        for j in range(2):
+            grouped = sb.tile([P, Q, PACK], BF16, name="grouped", align_bytes=64)
+            nc.vector.tensor_copy(
+                out=grouped[:].rearrange("p (c i) r -> p c r i", i=4),
+                in_=raw[j][:].rearrange("p r (c i) -> p c r i", i=4),
+            )
+            q_codes = sb.tile([P, Q], U32, name="q_codes%d" % j, align_bytes=64)
+            q_scales = sb.tile([P, Q], U8, name="q_scales%d" % j, align_bytes=64)
+            nc.vector.quantize_mx(
+                out=q_codes[:].bitcast(FP8X4), scales=q_scales[:], in_=grouped[:].rearrange("p q r -> p (q r)")
+            )
+            codes.append(q_codes)
+            scales.append(q_scales)
+
+        lam_wide = sb.tile([P, HALF], F32, name="lam_wide")
+        nc.scalar.activation(lam_wide[:], lam_col[:].to_broadcast([P, HALF]), COPY)
+
+        a = sb.tile([P, T], F32, name="grouped", align_bytes=64)
+        b = sb.tile([P, T], F32, name="b")
+        pieces = ((0, 512), (512, 768), (768, 1024))
+        for j, dst in enumerate((a, b)):
+            for n, (lo, hi) in enumerate(pieces):
+                bank = ps.tile([P, hi - lo], F32, name="bank%d_%d" % (j, n))
+                nc.tensor.matmul_mx(
+                    out=bank[:],
+                    lhsT=codes[j][:].bitcast(FP8X4),
+                    lhsT_scale=scales[j][:],
+                    rhs=key_words[:, lo:hi].bitcast(FP8X4),
+                    rhs_scale=key_scales[:, lo:hi],
+                    start=True,
+                    stop=True,
+                )
+                if j == 0 and n != 1:
+                    nc.scalar.activation(dst[:, lo:hi], bank[:], COPY)
+                else:
+                    nc.vector.tensor_copy(out=dst[:, lo:hi], in_=bank[:])
+
+        w = sb.tile([P, SLOTS], F32, name="w")
+        diff = sb.tile([P, SLOTS], F32, name="diff")
+        for c in range(2):
+            lo, hi = c * HALF, (c + 1) * HALF
+            a1 = sb.tile([P, HALF], F32, name="a1")
+            a2 = sb.tile([P, HALF], F32, name="a2")
+            b1 = sb.tile([P, HALF], F32, name="b1_%d" % c)
+            b2 = sb.tile([P, HALF], F32, name="b2_%d" % c)
+            if c == 0:
+                nc.scalar.activation(a1[:], a[:].indirect(cols(list1, lo, hi)), COPY)
+                nc.scalar.activation(a2[:], a[:].indirect(cols(list2, lo, hi)), COPY)
+                nc.vector.tensor_copy(b2[:], b[:].indirect(cols(list2, lo, hi)))
+                nc.scalar.activation(b1[:], b[:].indirect(cols(list1, lo, hi)), COPY)
+            else:
+                nc.scalar.activation(b2[:], b[:].indirect(cols(list2, lo, hi)), COPY)
+                nc.scalar.activation(b1[:], b[:].indirect(cols(list1, lo, hi)), COPY)
+                nc.scalar.activation(a1[:], a[:].indirect(cols(list1, lo, hi)), COPY)
+                nc.scalar.activation(a2[:], a[:].indirect(cols(list2, lo, hi)), COPY)
+            kept = sb.tile([P, HALF], F32, name="kept%d" % c)
+            exchanged = sb.tile([P, HALF], F32, name="exchanged%d" % c)
+            nc.vector.tensor_tensor(kept[:], a1[:], b2[:], ALU.max)
+            nc.vector.tensor_tensor(exchanged[:], a2[:], b1[:], ALU.max)
+            nc.vector.tensor_tensor(diff[:, lo:hi], kept[:], exchanged[:], ALU.subtract)
+            nc.vector.tensor_tensor(f1[:].indirect(cols(list1, lo, hi)), diff[:, lo:hi], lam_wide[:], ALU.mult)
+        nc.scalar.activation(w[:], diff[:], COPY, scale=lam_col[:])
+
+        f2 = sb.tile([P, T], F32, name="f2")
+        nc.vector.tensor_tensor(f2[:], f1[:], old_sb[:], ALU.add)
+
+        res0 = sb.tile([P, HALF], F32, name="res0")
+        res1 = sb.tile([P, HALF], F32, name="res1")
+        picked = sb.tile([P, HALF], F32, name="picked")
+        nc.scalar.activation(picked[:], f2[:].indirect(cols(list3, HALF, SLOTS)), COPY)
+        nc.vector.tensor_tensor(res0[:], f2[:].indirect(cols(list3, 0, HALF)), w[:, 0:HALF], ALU.mult)
+        nc.sync.dma_start(out=out[:, 0:HALF], in_=res0[:])
+        nc.vector.tensor_tensor(res1[:], picked[:], w[:, HALF:SLOTS], ALU.mult)
+        nc.scalar.dma_start(out=out[:, HALF:SLOTS], in_=res1[:])

@@ -16,6 +16,7 @@ P = 128
 PACK = 4
 D, T, SLOTS, Q = 512, 1024, 512, 128
 HALF = SLOTS // 2
+QUARTER = SLOTS // 4
 PER_COL = 16
 
 FLOPS = 2 * 2 * D * Q * T
@@ -30,36 +31,32 @@ def tile_attend_exchanged_lean_throughtimes_heads_kernel(
         ps = ctx.enter_context(tc.psum_pool(name="ps", bufs=1))
 
         raw = [sb.tile([P, PACK, Q], F32, name="raw%d" % j) for j in range(2)]
-        key_words = sb.tile([P, T], U32, name="key_words", align_bytes=64)
-        scale_rows = sb.tile([P, T // 4], U32, name="scale_rows")
+        key_words = [sb.tile([P, T // 2], U32, name="key_words%d" % j, align_bytes=64) for j in range(2)]
+        words = keys_words[0].rearrange("p n r -> p (n r)").bitcast(I32)
+        key_scales = sb.tile([P, T], U8, name="key_scales", align_bytes=64)
+        nc.gpsimd.memset(key_scales[:].bitcast(U32), 0)
         nc.sync.dma_start(out=raw[0][:], in_=query.rearrange("(p r) q -> p r q", r=PACK))
         for quad in range(4):
             nc.sync.dma_start(
-                out=scale_rows[32 * quad : 32 * quad + 4, :].bitcast(I32),
+                out=key_scales[32 * quad : 32 * quad + 4, :].bitcast(I32),
                 in_=keys_scales[0][4 * quad : 4 * quad + 4, :].bitcast(I32),
             )
-        nc.sync.dma_start(
-            out=key_words[:].bitcast(I32), in_=keys_words[0].rearrange("p n r -> p (n r)").bitcast(I32)
-        )
+        nc.sync.dma_start(out=key_words[0][:].bitcast(I32), in_=words[:, : T // 2])
         nc.sync.dma_start(out=raw[1][:], in_=query2.rearrange("(p r) q -> p r q", r=PACK))
+        nc.sync.dma_start(out=key_words[1][:].bitcast(I32), in_=words[:, T // 2 :])
         lam_col = sb.tile([P, 1], F32, name="lam_col")
         list1 = sb.tile([P, SLOTS // PER_COL], U16, name="list1")
         list2 = sb.tile([P, SLOTS // PER_COL], U16, name="list2")
         list3 = sb.tile([P, SLOTS // PER_COL], U16, name="list3")
         old_sb = sb.tile([P, T], F32, name="old_sb")
-        nc.sync.dma_start(out=lam_col[:], in_=lam)
-        nc.sync.dma_start(list1[:], offs)
         nc.sync.dma_start(list2[:], offs2)
+        nc.sync.dma_start(list1[:], offs)
+        nc.sync.dma_start(out=lam_col[:], in_=lam)
         nc.sync.dma_start(out=old_sb[:], in_=old)
         nc.sync.dma_start(list3[:], offs3)
 
-        key_scales = sb.tile([P, T], U8, name="key_scales", align_bytes=64)
-        nc.vector.memset(key_scales[:].bitcast(U32), 0)
         f1 = sb.tile([P, T], F32, name="f1")
         nc.vector.memset(f1[:], 0.0)
-        for quad in range(4):
-            rows = slice(32 * quad, 32 * quad + 4)
-            nc.vector.tensor_copy(out=key_scales[rows, :].bitcast(I32), in_=scale_rows[rows, :].bitcast(I32))
 
         def cols(lst, lo, hi):
             return lst[:, lo // PER_COL : hi // PER_COL]
@@ -79,12 +76,12 @@ def tile_attend_exchanged_lean_throughtimes_heads_kernel(
             codes.append(q_codes)
             scales.append(q_scales)
 
-        lam_wide = sb.tile([P, HALF], F32, name="lam_wide")
-        nc.scalar.activation(lam_wide[:], lam_col[:].to_broadcast([P, HALF]), COPY)
+        lam_wide = sb.tile([P, HALF], F32, name="grouped", align_bytes=64)
+        nc.vector.tensor_copy(out=lam_wide[:], in_=lam_col[:].to_broadcast([P, HALF]))
 
-        a = sb.tile([P, T], F32, name="grouped", align_bytes=64)
+        a = sb.tile([P, T], F32, name="a")
         b = sb.tile([P, T], F32, name="b")
-        pieces = ((0, 512), (512, 768), (768, 1024))
+        pieces = ((0, 256), (256, 512), (512, 768), (768, 1024))
         for j, dst in enumerate((a, b)):
             for n, (lo, hi) in enumerate(pieces):
                 bank = ps.tile([P, hi - lo], F32, name="bank%d_%d" % (j, n))
@@ -92,12 +89,12 @@ def tile_attend_exchanged_lean_throughtimes_heads_kernel(
                     out=bank[:],
                     lhsT=codes[j][:].bitcast(FP8X4),
                     lhsT_scale=scales[j][:],
-                    rhs=key_words[:, lo:hi].bitcast(FP8X4),
+                    rhs=key_words[n // 2][:, lo % 512 : lo % 512 + 256].bitcast(FP8X4),
                     rhs_scale=key_scales[:, lo:hi],
                     start=True,
                     stop=True,
                 )
-                if j == 0 and n != 1:
+                if j == 0 and n < 2:
                     nc.scalar.activation(dst[:, lo:hi], bank[:], COPY)
                 else:
                     nc.vector.tensor_copy(out=dst[:, lo:hi], in_=bank[:])
@@ -109,24 +106,29 @@ def tile_attend_exchanged_lean_throughtimes_heads_kernel(
             a1 = sb.tile([P, HALF], F32, name="a1")
             a2 = sb.tile([P, HALF], F32, name="a2")
             b1 = sb.tile([P, HALF], F32, name="b1_%d" % c)
-            b2 = sb.tile([P, HALF], F32, name="b2_%d" % c)
+            b2 = sb.tile([P, HALF], F32, name=("b2", "lam_col")[c])
             if c == 0:
                 nc.scalar.activation(a1[:], a[:].indirect(cols(list1, lo, hi)), COPY)
                 nc.scalar.activation(a2[:], a[:].indirect(cols(list2, lo, hi)), COPY)
                 nc.vector.tensor_copy(b2[:], b[:].indirect(cols(list2, lo, hi)))
                 nc.scalar.activation(b1[:], b[:].indirect(cols(list1, lo, hi)), COPY)
             else:
-                nc.scalar.activation(b2[:], b[:].indirect(cols(list2, lo, hi)), COPY)
                 nc.scalar.activation(b1[:], b[:].indirect(cols(list1, lo, hi)), COPY)
+                nc.scalar.activation(b2[:], b[:].indirect(cols(list2, lo, hi)), COPY)
                 nc.scalar.activation(a1[:], a[:].indirect(cols(list1, lo, hi)), COPY)
                 nc.scalar.activation(a2[:], a[:].indirect(cols(list2, lo, hi)), COPY)
-            kept = sb.tile([P, HALF], F32, name="kept%d" % c)
-            exchanged = sb.tile([P, HALF], F32, name="exchanged%d" % c)
-            nc.vector.tensor_tensor(kept[:], a1[:], b2[:], ALU.max)
-            nc.vector.tensor_tensor(exchanged[:], a2[:], b1[:], ALU.max)
-            nc.vector.tensor_tensor(diff[:, lo:hi], kept[:], exchanged[:], ALU.subtract)
+            kept = sb.tile([P, HALF], F32, name="kept")
+            exchanged = sb.tile([P, HALF], F32, name="exchanged")
+            parts = [slice(s, s + QUARTER) for s in (0, QUARTER)]
+            for part in parts:
+                nc.vector.tensor_tensor(kept[:, part], a1[:, part], b2[:, part], ALU.max)
+                nc.vector.tensor_tensor(exchanged[:, part], a2[:, part], b1[:, part], ALU.max)
+            for part in parts:
+                nc.vector.tensor_tensor(
+                    diff[:, lo + part.start : lo + part.stop], kept[:, part], exchanged[:, part], ALU.subtract
+                )
             nc.vector.tensor_tensor(f1[:].indirect(cols(list1, lo, hi)), diff[:, lo:hi], lam_wide[:], ALU.mult)
-        nc.scalar.activation(w[:], diff[:], COPY, scale=lam_col[:])
+        nc.scalar.activation(w[:], diff[:], COPY, scale=lam_wide[:, 0:1])
 
         f2 = sb.tile([P, T], F32, name="f2")
         nc.vector.tensor_tensor(f2[:], f1[:], old_sb[:], ALU.add)

from contextlib import ExitStack

import concourse.mybir as mybir

F32 = mybir.dt.float32
BF16 = mybir.dt.bfloat16
U32 = mybir.dt.uint32
I32 = mybir.dt.int32
U16 = mybir.dt.uint16
U8 = mybir.dt.uint8
FP8X4 = mybir.dt.float8_e4m3fn_x4
ALU = mybir.AluOpType
COPY = mybir.ActivationFunctionType.Copy

P = 128
PACK = 4
D, T, SLOTS, Q = 512, 1024, 512, 128
HALF = SLOTS // 2
QUARTER = SLOTS // 4
PER_COL = 16

FLOPS = 2 * 2 * D * Q * T


def tile_attend_exchanged_lean_throughtimes_heads_kernel(
    tc, query, query2, keys_words, keys_scales, lam, old, offs, offs2, offs3, out
):
    nc = tc.nc
    with ExitStack() as ctx:
        sb = ctx.enter_context(tc.tile_pool(name="sb", bufs=1))
        ps = ctx.enter_context(tc.psum_pool(name="ps", bufs=1))

        raw = [sb.tile([P, PACK, Q], F32, name="raw%d" % j) for j in range(2)]
        key_words = [sb.tile([P, T // 2], U32, name="key_words%d" % j, align_bytes=64) for j in range(2)]
        words = keys_words[0].rearrange("p n r -> p (n r)").bitcast(I32)
        key_scales = sb.tile([P, T], U8, name="key_scales", align_bytes=64)
        nc.gpsimd.memset(key_scales[:].bitcast(U32), 0)
        nc.sync.dma_start(out=raw[0][:], in_=query.rearrange("(p r) q -> p r q", r=PACK))
        for quad in range(4):
            nc.sync.dma_start(
                out=key_scales[32 * quad : 32 * quad + 4, :].bitcast(I32),
                in_=keys_scales[0][4 * quad : 4 * quad + 4, :].bitcast(I32),
            )
        nc.sync.dma_start(out=key_words[0][:].bitcast(I32), in_=words[:, : T // 2])
        nc.sync.dma_start(out=raw[1][:], in_=query2.rearrange("(p r) q -> p r q", r=PACK))
        nc.sync.dma_start(out=key_words[1][:].bitcast(I32), in_=words[:, T // 2 :])
        lam_col = sb.tile([P, 1], F32, name="lam_col")
        list1 = sb.tile([P, SLOTS // PER_COL], U16, name="list1")
        list2 = sb.tile([P, SLOTS // PER_COL], U16, name="list2")
        list3 = sb.tile([P, SLOTS // PER_COL], U16, name="list3")
        old_sb = sb.tile([P, T], F32, name="old_sb")
        nc.sync.dma_start(list2[:], offs2)
        nc.sync.dma_start(list1[:], offs)
        nc.sync.dma_start(out=lam_col[:], in_=lam)
        nc.sync.dma_start(out=old_sb[:], in_=old)
        nc.sync.dma_start(list3[:], offs3)

        f1 = sb.tile([P, T], F32, name="f1")
        nc.vector.memset(f1[:], 0.0)

        def cols(lst, lo, hi):
            return lst[:, lo // PER_COL : hi // PER_COL]

        codes, scales = [], []
        for j in range(2):
            grouped = sb.tile([P, Q, PACK], BF16, name="grouped", align_bytes=64)
            nc.vector.tensor_copy(
                out=grouped[:].rearrange("p (c i) r -> p c r i", i=4),
                in_=raw[j][:].rearrange("p r (c i) -> p c r i", i=4),
            )
            q_codes = sb.tile([P, Q], U32, name="q_codes%d" % j, align_bytes=64)
            q_scales = sb.tile([P, Q], U8, name="q_scales%d" % j, align_bytes=64)
            nc.vector.quantize_mx(
                out=q_codes[:].bitcast(FP8X4), scales=q_scales[:], in_=grouped[:].rearrange("p q r -> p (q r)")
            )
            codes.append(q_codes)
            scales.append(q_scales)

        lam_wide = sb.tile([P, HALF], F32, name="grouped", align_bytes=64)
        nc.vector.tensor_copy(out=lam_wide[:], in_=lam_col[:].to_broadcast([P, HALF]))

        a = sb.tile([P, T], F32, name="a")
        b = sb.tile([P, T], F32, name="b")
        pieces = ((0, 256), (256, 512), (512, 768), (768, 1024))
        for j, dst in enumerate((a, b)):
            for n, (lo, hi) in enumerate(pieces):
                bank = ps.tile([P, hi - lo], F32, name="bank%d_%d" % (j, n))
                nc.tensor.matmul_mx(
                    out=bank[:],
                    lhsT=codes[j][:].bitcast(FP8X4),
                    lhsT_scale=scales[j][:],
                    rhs=key_words[n // 2][:, lo % 512 : lo % 512 + 256].bitcast(FP8X4),
                    rhs_scale=key_scales[:, lo:hi],
                    start=True,
                    stop=True,
                )
                if j == 0 and n < 2:
                    nc.scalar.activation(dst[:, lo:hi], bank[:], COPY)
                else:
                    nc.vector.tensor_copy(out=dst[:, lo:hi], in_=bank[:])

        w = sb.tile([P, SLOTS], F32, name="w")
        diff = sb.tile([P, SLOTS], F32, name="diff")
        for c in range(2):
            lo, hi = c * HALF, (c + 1) * HALF
            a1 = sb.tile([P, HALF], F32, name="a1")
            a2 = sb.tile([P, HALF], F32, name="a2")
            b1 = sb.tile([P, HALF], F32, name="b1_%d" % c)
            b2 = sb.tile([P, HALF], F32, name=("b2", "lam_col")[c])
            if c == 0:
                nc.scalar.activation(a1[:], a[:].indirect(cols(list1, lo, hi)), COPY)
                nc.scalar.activation(a2[:], a[:].indirect(cols(list2, lo, hi)), COPY)
                nc.vector.tensor_copy(b2[:], b[:].indirect(cols(list2, lo, hi)))
                nc.scalar.activation(b1[:], b[:].indirect(cols(list1, lo, hi)), COPY)
            else:
                nc.scalar.activation(b1[:], b[:].indirect(cols(list1, lo, hi)), COPY)
                nc.scalar.activation(b2[:], b[:].indirect(cols(list2, lo, hi)), COPY)
                nc.scalar.activation(a1[:], a[:].indirect(cols(list1, lo, hi)), COPY)
                nc.scalar.activation(a2[:], a[:].indirect(cols(list2, lo, hi)), COPY)
            kept = sb.tile([P, HALF], F32, name="kept")
            exchanged = sb.tile([P, HALF], F32, name="exchanged")
            parts = [slice(s, s + QUARTER) for s in (0, QUARTER)]
            for part in parts:
                nc.vector.tensor_tensor(kept[:, part], a1[:, part], b2[:, part], ALU.max)
                nc.vector.tensor_tensor(exchanged[:, part], a2[:, part], b1[:, part], ALU.max)
            for part in parts:
                nc.vector.tensor_tensor(
                    diff[:, lo + part.start : lo + part.stop], kept[:, part], exchanged[:, part], ALU.subtract
                )
            nc.vector.tensor_tensor(f1[:].indirect(cols(list1, lo, hi)), diff[:, lo:hi], lam_wide[:], ALU.mult)
        nc.scalar.activation(w[:], diff[:], COPY, scale=lam_wide[:, 0:1])

        f2 = sb.tile([P, T], F32, name="f2")
        nc.vector.tensor_tensor(f2[:], f1[:], old_sb[:], ALU.add)

        res0 = sb.tile([P, HALF], F32, name="res0")
        res1 = sb.tile([P, HALF], F32, name="res1")
        picked = sb.tile([P, HALF], F32, name="picked")
        nc.scalar.activation(picked[:], f2[:].indirect(cols(list3, HALF, SLOTS)), COPY)
        nc.vector.tensor_tensor(res0[:], f2[:].indirect(cols(list3, 0, HALF)), w[:, 0:HALF], ALU.mult)
        nc.sync.dma_start(out=out[:, 0:HALF], in_=res0[:])
        nc.vector.tensor_tensor(res1[:], picked[:], w[:, HALF:SLOTS], ALU.mult)
        nc.scalar.dma_start(out=out[:, HALF:SLOTS], in_=res1[:])
